import numpy as np
import ml_dtypes


def mxq(x, axis, fmt="e4m3"):
    dtype, down = {"e4m3": (ml_dtypes.float8_e4m3fn, 7), "e5m2": (ml_dtypes.float8_e5m2, 14)}[fmt]
    v = np.moveaxis(np.asarray(x, np.float32).astype(ml_dtypes.bfloat16).astype(np.float64), axis, -1)
    blocks = v.reshape(v.shape[:-1] + (-1, 32))
    amax = np.abs(blocks).max(-1, keepdims=True)
    byte = np.maximum(np.where(amax > 0, np.frexp(amax)[1] - 1 + 127, 0) - down, 1)
    scale = np.exp2(byte - 127.0)
    codes = (blocks / scale).astype(np.float32).astype(dtype).astype(np.float64)
    return np.moveaxis((codes * scale).reshape(v.shape), -1, axis)


WIDE = False


def mx_kscale(k):
    if not WIDE:
        return np.ones(k)
    levels = np.array([10, -10, 5, -5, 0])
    if k % 512:
        return np.exp2(np.random.permutation(np.resize(levels, k // 32))).repeat(32)
    a = np.empty((k // 512, 16))
    for p in range(k // 512):
        a[p, :8] = np.random.permutation(np.resize(levels, 8))
        for g in range(8):
            far = levels[np.abs(levels - a[p, g]) >= 10]
            a[p, g + 8] = far[np.random.randint(len(far))]
    return np.exp2(a.ravel()).repeat(32)


def f64(x):
    return np.asarray(x).astype(np.float64)


def striped8(idx):
    return np.asarray(idx).reshape(8, -1, 16).transpose(0, 2, 1).reshape(128, -1).astype(np.uint16)


def unstriped8(offs):
    return offs.reshape(8, 16, -1).transpose(0, 2, 1).reshape(8, -1).astype(np.int64)


def pick8(x, idx, run):
    r = np.arange(len(x))
    return x[r[:, None], idx[r % (8 * run) // run]]


E2M1 = np.array([0.0, 0.5, 1.0, 1.5, 2.0, 3.0, 4.0, 6.0, -0.0, -0.5, -1.0, -1.5, -2.0, -3.0, -4.0, -6.0])


def pack_weight(w, fmt):
    k, n = w.shape
    w = f64(np.asarray(w, np.float32).astype(ml_dtypes.bfloat16)).reshape(k // 32, 32, n)
    amax = np.abs(w).max(1)
    if fmt == "e4m3":
        byte = np.frexp(amax)[1] - 1 + 127 - 7
    else:
        mant, ex = np.frexp(amax / 6.0)
        byte = np.where(mant > 0.5, ex, ex - 1) + 127
    byte = np.clip(np.where(amax > 0, byte, 1), 1, 254)
    scaled = (w * np.exp2(127.0 - byte)[:, None, :]).reshape(k, n).astype(np.float32)
    by_word = np.ascontiguousarray(scaled.reshape(k // 512, 128, 4, n).transpose(0, 1, 3, 2))
    if fmt == "e4m3":
        words = by_word.astype(ml_dtypes.float8_e4m3fn).view(np.uint8)
    else:
        c = by_word.astype(ml_dtypes.float4_e2m1fn).view(np.uint8) & 0xF
        words = (c[..., 0::2] | (c[..., 1::2] << 4)).reshape(k // 512, 128, 2 * n)
    return np.ascontiguousarray(words), np.ascontiguousarray(byte.astype(np.uint8).reshape(k // 512, 16, n))


def unpack_weight(words, scales, fmt):
    g, _, n = scales.shape
    words = np.ascontiguousarray(words).reshape(g, 128, n, -1)
    if fmt == "e4m3":
        vals = words.view(ml_dtypes.float8_e4m3fn).astype(np.float64)
    else:
        nib = np.empty((g, 128, n, 4), np.uint8)
        nib[..., 0::2] = words & 0xF
        nib[..., 1::2] = words >> 4
        vals = E2M1[nib]
    vals = vals * np.repeat(np.exp2(scales.astype(np.float64) - 127.0), 8, axis=1)[..., None]
    return vals.transpose(0, 1, 3, 2).reshape(g * 512, n)


C, D, I, Z, J, Q = 512, 512, 256, 512, 256, 128


def setup_inputs():
    n = np.random.standard_normal
    idx = np.stack([np.random.permutation(Z)[:I] for _ in range(8)])
    idx2 = np.stack([np.random.permutation(Z)[:I] for _ in range(8)])
    idx3 = np.stack([np.random.permutation(Z)[:J] for _ in range(8)])
    idx4 = np.stack([np.random.permutation(Z)[:J] for _ in range(8)])
    idx5 = np.stack([np.random.permutation(Z)[:J] for _ in range(8)])
    fc = mx_kscale(C)
    fd = mx_kscale(D)
    wpp = pack_weight(n((C, D)) * 1.0 / np.sqrt(C) * fc[:, None] / fd, "e4m3")
    oldsp = pack_weight(n((C, Z)) / fc[:, None], "e2m1")
    wkp = pack_weight(n((C, D)) * 1.0 / np.sqrt(C) * fc[:, None] / fd, "e2m1")
    newsp = pack_weight(n((C, I)) / fc[:, None], "e4m3")
    wlp = pack_weight(n((C, D)) * 1.0 / np.sqrt(C) * fc[:, None] / fd, "e4m3")
    latesp = pack_weight(n((C, I)) / fc[:, None], "e2m1")
    return {
        "wp_words": wpp[0],
        "wp_scales": wpp[1],
        "olds_words": oldsp[0],
        "olds_scales": oldsp[1],
        "wk_words": wkp[0],
        "wk_scales": wkp[1],
        "news_words": newsp[0],
        "news_scales": newsp[1],
        "wl_words": wlp[0],
        "wl_scales": wlp[1],
        "lates_words": latesp[0],
        "lates_scales": latesp[1],
        "query": (n((D, Q)) * 1.0 / np.sqrt(D) * fd[:, None]).astype(np.float32),
        "offs": striped8(idx),
        "offs2": striped8(idx2),
        "offs3": striped8(idx3),
        "offs4": striped8(idx4),
        "offs5": striped8(idx5),
    }


def reference(wp_words, wp_scales, olds_words, olds_scales, wk_words, wk_scales, news_words, news_scales, wl_words, wl_scales, lates_words, lates_scales, query, offs, offs2, offs3, offs4, offs5):
    idx = unstriped8(offs)
    idx2 = unstriped8(offs2)
    idx3 = unstriped8(offs3)
    idx4 = unstriped8(offs4)
    idx5 = unstriped8(offs5)
    wpu = unpack_weight(wp_words, wp_scales, "e4m3")
    oldsu = unpack_weight(olds_words, olds_scales, "e2m1")
    wku = unpack_weight(wk_words, wk_scales, "e2m1")
    newsu = unpack_weight(news_words, news_scales, "e4m3")
    wlu = unpack_weight(wl_words, wl_scales, "e4m3")
    latesu = unpack_weight(lates_words, lates_scales, "e2m1")
    kb = wpu.T @ oldsu
    kn = wku.T @ newsu
    km = wlu.T @ latesu
    f1 = np.zeros((D, Z))
    f1[np.arange(D)[:, None], idx[np.arange(D) % 512 // 64]] = kn
    f2 = np.zeros((D, Z))
    f2[np.arange(D)[:, None], idx2[np.arange(D) % 512 // 64]] = km
    m1 = np.maximum(kb, f1)
    pg = m1 - f2
    queryq = mxq(f64(query), 0, "e4m3")
    pgq = mxq(pg, 0, "e4m3")
    s = queryq.T @ pgq
    f3 = np.zeros((Q, Z))
    f3[np.arange(Q)[:, None], idx4[np.arange(Q) % 128 // 16]] = pick8(s, idx3, 16)
    y = np.maximum(pick8(f3, idx5, 16), pick8(s, idx3, 16))
    return y

@@ -1,0 +1,191 @@
+from contextlib import ExitStack
+
+import concourse.mybir as mybir
+
+C, D, I, Z, J, Q = 512, 512, 256, 512, 256, 128
+FLOPS = 2 * C * D * (Z + I + I) + 2 * D * Q * Z
+
+F32 = mybir.dt.float32
+BF16 = mybir.dt.bfloat16
+I32 = mybir.dt.int32
+U32 = mybir.dt.uint32
+U16 = mybir.dt.uint16
+U8 = mybir.dt.uint8
+FP8X4 = mybir.dt.float8_e4m3fn_x4
+FP4X4 = mybir.dt.float4_e2m1fn_x4
+COPY = mybir.ActivationFunctionType.Copy
+MAX = mybir.AluOpType.max
+SUB = mybir.AluOpType.subtract
+
+P = 128
+PACK = 4
+QUADS = 4
+HALF = Z // 2
+
+
+def tile_attend_headmeet_plainq_kernel(tc, wp_words, wp_scales, olds_words, olds_scales, wk_words, wk_scales,
+                                        news_words, news_scales, wl_words, wl_scales, lates_words, lates_scales,
+                                        query, offs, offs2, offs3, offs4, offs5, out):
+    nc = tc.nc
+    with ExitStack() as ctx:
+        sb = ctx.enter_context(tc.tile_pool(name="sb", bufs=1))
+        ps = ctx.enter_context(tc.psum_pool(name="ps", bufs=1))
+
+        def held(name, shape, dtype):
+            return sb.tile(shape, dtype, name=name, align_bytes=64)
+
+        def load_list(name, src):
+            lst = held(name, [P, 16], U16)
+            nc.sync.dma_start(lst[:], src)
+            return lst
+
+        def load_words(name, src):
+            words = held(name, [P, src.shape[1]], U8)
+            nc.sync.dma_start(words[:].bitcast(I32), src.bitcast(I32))
+            return words
+
+        def dealt(ap):
+            return ap.rearrange("p (g t w) -> p t g w", g=32, t=PACK)
+
+        def by_place(ap):
+            return ap.rearrange("p (t g w) -> p t g w", g=32, t=PACK)
+
+        def deal(name, src):
+            dst = held(name, [P, src.shape[1]], U8)
+            nc.vector.tensor_copy(by_place(dst[:].bitcast(I32)), dealt(src[:].bitcast(I32)))
+            return dst
+
+        def zeroed(name, width, dtype):
+            t = held(name, [P, width], dtype)
+            if dtype == U8:
+                nc.vector.memset(t[:].bitcast(I32), 0)
+            else:
+                nc.vector.memset(t[:], 0.0)
+            return t
+
+        def load_staged_scales(name, src):
+            stage = held(name, [4, QUADS, src.shape[1] // 4], I32)
+            nc.sync.dma_start(stage[:], src.bitcast(I32).rearrange("(u f) w -> f u w", f=4))
+            return stage
+
+        def load_scales(plane, src):
+            for u in range(QUADS):
+                nc.sync.dma_start(plane[32 * u: 32 * u + 4, :].bitcast(I32), src[4 * u: 4 * u + 4, :].bitcast(I32))
+
+        def e4m3_rows(words):
+            return words[0].rearrange("p n r -> p (n r)")
+
+        news_plane = zeroed("news_plane", I, U8)
+        list1 = load_list("list1", offs)
+        wk_stage = load_staged_scales("wk_stage", wk_scales[0])
+        wk_raw = load_words("wk_raw", wk_words[0])
+        load_scales(news_plane, news_scales[0])
+        news_w = load_words("news_w", e4m3_rows(news_words))
+
+        wk_plane = zeroed("wk_plane", D, U8)
+        f1 = [zeroed("f1_%d" % t, Z, F32) for t in range(PACK)]
+        for u in range(QUADS):
+            rows = slice(32 * u, 32 * u + 4)
+            nc.vector.tensor_copy(by_place(wk_plane[rows, :].bitcast(I32)), dealt(wk_stage[:, u, :]))
+        wk_w = deal("wk_w", wk_raw)
+
+        def keys(name, t, w_words, w_dtype, w_plane, x_words, x_dtype, x_plane, width, tag):
+            per = w_words.shape[1] // PACK
+            acc = ps.tile([P, width], F32, name="%s_%d" % (name, t), tag=tag)
+            nc.tensor.matmul_mx(out=acc[:], lhsT=w_words[:, t * per:(t + 1) * per].bitcast(w_dtype),
+                                lhsT_scale=w_plane[:, t * P:(t + 1) * P],
+                                rhs=x_words[:].bitcast(x_dtype), rhs_scale=x_plane[:], start=True, stop=True)
+            return acc
+
+        for t in range(PACK):
+            acc = keys("kn_ps", t, wk_w, FP4X4, wk_plane, news_w, FP8X4, news_plane, I, "small%d" % (t % 2))
+            kn = held("kn_%d" % t, [P, I], F32)
+            nc.vector.tensor_copy(kn[:], acc[:])
+            nc.scalar.activation(f1[t][:].indirect(list1[:]), kn[:], COPY)
+
+        wl_raw = load_words("wl_raw", e4m3_rows(wl_words))
+        lates_w = load_words("lates_w", lates_words[0])
+        list2 = load_list("list2", offs2)
+        wl_plane_raw = zeroed("wl_plane_raw", D, U8)
+        lates_plane = zeroed("lates_plane", I, U8)
+        load_scales(wl_plane_raw, wl_scales[0])
+        load_scales(lates_plane, lates_scales[0])
+
+        q_raw = held("q_raw", [P, PACK, Q], F32)
+        q_rows = query.rearrange("(g t e) q -> e g t q", t=PACK, e=4)
+        for e in range(4):
+            nc.sync.dma_start(q_raw[e:P:4, :, :], q_rows[e])
+
+        wp_raw = load_words("wp_raw", e4m3_rows(wp_words))
+        olds_w = load_words("olds_w", olds_words[0])
+        wp_plane_raw = zeroed("wp_plane_raw", D, U8)
+        olds_plane = zeroed("olds_plane", Z, U8)
+        load_scales(wp_plane_raw, wp_scales[0])
+        load_scales(olds_plane, olds_scales[0])
+        list3 = load_list("list3", offs3)
+        list4 = load_list("list4", offs4)
+        list5 = load_list("list5", offs5)
+
+        wl_w = deal("wl_w", wl_raw)
+        wl_plane = deal("wl_plane", wl_plane_raw)
+        f2 = [zeroed("f2_%d" % t, Z, F32) for t in range(PACK)]
+        km = []
+        for t in range(PACK):
+            acc = keys("km_ps", t, wl_w, FP8X4, wl_plane, lates_w, FP4X4, lates_plane, I, "small%d" % (t % 2))
+            km.append(held("km_%d" % t, [P, I], F32))
+            nc.vector.tensor_copy(km[t][:], acc[:])
+
+        q_bf = held("q_bf", [P, Q, PACK], BF16)
+        nc.vector.tensor_copy(q_bf[:], q_raw[:].rearrange("p t q -> p q t"))
+        wp_w = deal("wp_w", wp_raw)
+        q_codes = held("q_codes", [P, Q], U32)
+        q_plane = held("q_plane", [P, Q], U8)
+        nc.vector.quantize_mx(out=q_codes[:].bitcast(FP8X4), scales=q_plane[:],
+                              in_=q_bf[:].rearrange("p q t -> p (q t)"))
+        wp_plane = deal("wp_plane", wp_plane_raw)
+        f3 = zeroed("f3", Z, F32)
+
+        m1 = []
+        for t in range(PACK):
+            acc = keys("kb_ps", t, wp_w, FP8X4, wp_plane, olds_w, FP4X4, olds_plane, Z, "big%d" % t)
+            m1.append(held("m1_%d" % t, [P, Z], F32))
+            nc.vector.tensor_tensor(m1[t][:], acc[:], f1[t][:], MAX)
+
+        pairs = [held("pairs_%d" % h, [P, 2, HALF, 2], BF16) for h in range(2)]
+        for t in range(PACK):
+            nc.scalar.activation(f2[t][:].indirect(list2[:]), km[t][:], COPY)
+            for h in range(2):
+                zs = slice(h * HALF, (h + 1) * HALF)
+                nc.vector.tensor_tensor(pairs[h][:, t // 2, :, t % 2], m1[t][:, zs], f2[t][:, zs], SUB)
+
+        pg_bf = [held("pg_bf_%d" % h, [P, HALF * PACK], BF16) for h in range(2)]
+        for h in range(2):
+            nc.vector.tensor_copy(
+                pg_bf[h][:].bitcast(F32).rearrange("p (z u) -> p z u", u=2),
+                pairs[h][:].rearrange("p u z e -> p (u z e)").bitcast(F32).rearrange("p (u z) -> p z u", u=2))
+        scores = held("scores", [P, Z], F32)
+        for h in range(2):
+            codes = held("pg_codes_%d" % h, [P, HALF], U32)
+            plane = held("pg_plane_%d" % h, [P, HALF], U8)
+            nc.vector.quantize_mx(out=codes[:].bitcast(FP8X4), scales=plane[:], in_=pg_bf[h][:])
+            acc = ps.tile([P, HALF], F32, name="s_ps_%d" % h, tag="score%d" % h)
+            nc.tensor.matmul_mx(out=acc[:], lhsT=q_codes[:].bitcast(FP8X4), lhsT_scale=q_plane[:],
+                                rhs=codes[:].bitcast(FP8X4), rhs_scale=plane[:], start=True, stop=True)
+            zs = slice(h * HALF, (h + 1) * HALF)
+            if h == 0:
+                nc.scalar.copy(scores[:, zs], acc[:])
+            else:
+                nc.vector.tensor_copy(scores[:, zs], acc[:])
+
+        cols = J // 2 // 16
+        picked = [held("picked_%d" % h, [P, J // 2], F32) for h in range(2)]
+        for h in range(2):
+            nc.vector.tensor_copy(picked[h][:], scores[:].indirect(list3[:, h * cols:(h + 1) * cols]))
+            nc.scalar.activation(f3[:].indirect(list4[:, h * cols:(h + 1) * cols]), picked[h][:], COPY)
+        met = [held("met_%d" % h, [P, J // 2], F32) for h in range(2)]
+        nc.vector.tensor_copy(met[0][:], f3[:].indirect(list5[:, 0:cols]))
+        nc.scalar.activation(met[1][:], f3[:].indirect(list5[:, cols:2 * cols]), COPY)
+        result = held("result", [P, J], F32)
+        for h in range(2):
+            nc.vector.tensor_tensor(result[:, h * (J // 2):(h + 1) * (J // 2)], met[h][:], picked[h][:], MAX)
+        nc.sync.dma_start(out, result[:])

@@ -20,7 +20,8 @@ SUB = mybir.AluOpType.subtract
 P = 128
 PACK = 4
 QUADS = 4
-HALF = Z // 2
+PARTS = 4
+PART = Z // PARTS
 
 
 def tile_attend_headmeet_plainq_kernel(tc, wp_words, wp_scales, olds_words, olds_scales, wk_words, wk_scales,
@@ -31,8 +32,8 @@ def tile_attend_headmeet_plainq_kernel(tc, wp_words, wp_scales, olds_words, olds
         sb = ctx.enter_context(tc.tile_pool(name="sb", bufs=1))
         ps = ctx.enter_context(tc.psum_pool(name="ps", bufs=1))
 
-        def held(name, shape, dtype):
-            return sb.tile(shape, dtype, name=name, align_bytes=64)
+        def held(name, shape, dtype, tag=""):
+            return sb.tile(shape, dtype, name=name, tag=tag or name, align_bytes=64)
 
         def load_list(name, src):
             lst = held(name, [P, 16], U16)
@@ -47,20 +48,17 @@ def tile_attend_headmeet_plainq_kernel(tc, wp_words, wp_scales, olds_words, olds
         def dealt(ap):
             return ap.rearrange("p (g t w) -> p t g w", g=32, t=PACK)
 
-        def by_place(ap):
-            return ap.rearrange("p (t g w) -> p t g w", g=32, t=PACK)
+        def by_place(ap, places=PACK):
+            return ap.rearrange("p (t g w) -> p t g w", g=32, t=places)
 
         def deal(name, src):
             dst = held(name, [P, src.shape[1]], U8)
             nc.vector.tensor_copy(by_place(dst[:].bitcast(I32)), dealt(src[:].bitcast(I32)))
             return dst
 
-        def zeroed(name, width, dtype):
-            t = held(name, [P, width], dtype)
-            if dtype == U8:
-                nc.vector.memset(t[:].bitcast(I32), 0)
-            else:
-                nc.vector.memset(t[:], 0.0)
+        def zeroed(name, width, dtype, tag="", engine=nc.gpsimd):
+            t = held(name, [P, width], dtype, tag)
+            engine.memset(t[:].bitcast(I32), 0)
             return t
 
         def load_staged_scales(name, src):
@@ -75,30 +73,40 @@ def tile_attend_headmeet_plainq_kernel(tc, wp_words, wp_scales, olds_words, olds
         def e4m3_rows(words):
             return words[0].rearrange("p n r -> p (n r)")
 
-        news_plane = zeroed("news_plane", I, U8)
-        list1 = load_list("list1", offs)
+        warm = held("warm", [P, 16], F32)
+        nc.vector.memset(warm[:, 0:8], 0.0)
+        nc.scalar.activation(warm[:, 8:16], warm[:, 0:8], COPY)
+        news_plane = zeroed("news_plane", 2 * I, U8)
         wk_stage = load_staged_scales("wk_stage", wk_scales[0])
+        news_rows = news_scales[0].bitcast(I32).rearrange("(v u f) w -> u f v w", v=2, u=2)
+        for u in range(2):
+            nc.sync.dma_start(news_plane[32 * u:32 * u + 4, :].bitcast(I32).rearrange("f (v w) -> f v w", v=2),
+                                news_rows[u])
         wk_raw = load_words("wk_raw", wk_words[0])
-        load_scales(news_plane, news_scales[0])
         news_w = load_words("news_w", e4m3_rows(news_words))
+        list1 = load_list("list1", offs)
 
-        wk_plane = zeroed("wk_plane", D, U8)
-        f1 = [zeroed("f1_%d" % t, Z, F32) for t in range(PACK)]
+        wk_plane = zeroed("wk_plane", D, U8, engine=nc.vector)
+        f1 = [zeroed("f1_%d" % t, Z, F32, engine=nc.vector) for t in range(2)]
         for u in range(QUADS):
             rows = slice(32 * u, 32 * u + 4)
-            nc.vector.tensor_copy(by_place(wk_plane[rows, :].bitcast(I32)), dealt(wk_stage[:, u, :]))
-        wk_w = deal("wk_w", wk_raw)
+            move, word = (nc.scalar.copy, U32) if u == 0 else (nc.vector.tensor_copy, I32)
+            move(by_place(wk_plane[rows, :].bitcast(word)), dealt(wk_stage[:, u, :].bitcast(word)))
+        nc.vector.tensor_copy(news_plane[64:P, 0:I].bitcast(I32), news_plane[0:64, I:2 * I].bitcast(I32))
+        wk_w = held("wk_w", [P, 2 * D], U8)
+        nc.scalar.copy(by_place(wk_w[:].bitcast(U32)), dealt(wk_raw[:].bitcast(U32)))
+        f1.append(zeroed("f1_2", Z, F32, "wk_raw"))
+        f1.append(zeroed("f1_3", Z, F32, "wk_stage"))
 
-        def keys(name, t, w_words, w_dtype, w_plane, x_words, x_dtype, x_plane, width, tag):
-            per = w_words.shape[1] // PACK
-            acc = ps.tile([P, width], F32, name="%s_%d" % (name, t), tag=tag)
-            nc.tensor.matmul_mx(out=acc[:], lhsT=w_words[:, t * per:(t + 1) * per].bitcast(w_dtype),
+        def keys(acc, t, w_words, w_dtype, w_plane, x_words, x_dtype, x_plane):
+            per = P * w_words.shape[1] // w_plane.shape[1]
+            nc.tensor.matmul_mx(out=acc, lhsT=w_words[:, t * per:(t + 1) * per].bitcast(w_dtype),
                                 lhsT_scale=w_plane[:, t * P:(t + 1) * P],
-                                rhs=x_words[:].bitcast(x_dtype), rhs_scale=x_plane[:], start=True, stop=True)
-            return acc
+                                rhs=x_words[:].bitcast(x_dtype), rhs_scale=x_plane, start=True, stop=True)
 
         for t in range(PACK):
-            acc = keys("kn_ps", t, wk_w, FP4X4, wk_plane, news_w, FP8X4, news_plane, I, "small%d" % (t % 2))
+            acc = ps.tile([P, I], F32, name="kn_ps_%d" % t, tag="small%d" % (t % 2))
+            keys(acc[:], t, wk_w, FP4X4, wk_plane, news_w, FP8X4, news_plane[:, 0:I])
             kn = held("kn_%d" % t, [P, I], F32)
             nc.vector.tensor_copy(kn[:], acc[:])
             nc.scalar.activation(f1[t][:].indirect(list1[:]), kn[:], COPY)
@@ -128,12 +136,15 @@ def tile_attend_headmeet_plainq_kernel(tc, wp_words, wp_scales, olds_words, olds
 
         wl_w = deal("wl_w", wl_raw)
         wl_plane = deal("wl_plane", wl_plane_raw)
-        f2 = [zeroed("f2_%d" % t, Z, F32) for t in range(PACK)]
+        f2 = [zeroed("f2_%d" % t, Z, F32, "kn_%d" % t) for t in range(PACK)]
         km = []
-        for t in range(PACK):
-            acc = keys("km_ps", t, wl_w, FP8X4, wl_plane, lates_w, FP4X4, lates_plane, I, "small%d" % (t % 2))
-            km.append(held("km_%d" % t, [P, I], F32))
-            nc.vector.tensor_copy(km[t][:], acc[:])
+        for u in range(2):
+            bank = ps.tile([P, 2 * I], F32, name="km_ps_%d" % u, tag="late%d" % u)
+            for e in range(2):
+                keys(bank[:, e * I:(e + 1) * I], 2 * u + e, wl_w, FP8X4, wl_plane, lates_w, FP4X4, lates_plane[:])
+            km_pair = held("km_%d" % u, [P, 2 * I], F32)
+            nc.vector.tensor_copy(km_pair[:], bank[:])
+            km.extend([km_pair[:, 0:I], km_pair[:, I:2 * I]])
 
         q_bf = held("q_bf", [P, Q, PACK], BF16)
         nc.vector.tensor_copy(q_bf[:], q_raw[:].rearrange("p t q -> p q t"))
@@ -143,49 +154,53 @@ def tile_attend_headmeet_plainq_kernel(tc, wp_words, wp_scales, olds_words, olds
         nc.vector.quantize_mx(out=q_codes[:].bitcast(FP8X4), scales=q_plane[:],
                               in_=q_bf[:].rearrange("p q t -> p (q t)"))
         wp_plane = deal("wp_plane", wp_plane_raw)
-        f3 = zeroed("f3", Z, F32)
+        f3 = zeroed("f3", Z, F32, "news_w")
 
         m1 = []
         for t in range(PACK):
-            acc = keys("kb_ps", t, wp_w, FP8X4, wp_plane, olds_w, FP4X4, olds_plane, Z, "big%d" % t)
+            acc = ps.tile([P, Z], F32, name="kb_ps_%d" % t, tag="big%d" % t)
+            keys(acc[:], t, wp_w, FP8X4, wp_plane, olds_w, FP4X4, olds_plane[:])
             m1.append(held("m1_%d" % t, [P, Z], F32))
             nc.vector.tensor_tensor(m1[t][:], acc[:], f1[t][:], MAX)
 
-        pairs = [held("pairs_%d" % h, [P, 2, HALF, 2], BF16) for h in range(2)]
+        pairs = [held("pairs_%d" % h, [P, 2, PART, 2], BF16) for h in range(PARTS)]
         for t in range(PACK):
-            nc.scalar.activation(f2[t][:].indirect(list2[:]), km[t][:], COPY)
-            for h in range(2):
-                zs = slice(h * HALF, (h + 1) * HALF)
+            nc.scalar.activation(f2[t][:].indirect(list2[:]), km[t], COPY)
+            for h in range(PARTS):
+                zs = slice(h * PART, (h + 1) * PART)
                 nc.vector.tensor_tensor(pairs[h][:, t // 2, :, t % 2], m1[t][:, zs], f2[t][:, zs], SUB)
 
-        pg_bf = [held("pg_bf_%d" % h, [P, HALF * PACK], BF16) for h in range(2)]
-        for h in range(2):
-            nc.vector.tensor_copy(
+        pg_bf = [held("pg_bf_%d" % h, [P, PART * PACK], BF16) for h in range(PARTS)]
+        for h in range(PARTS):
+            interleave = nc.scalar.copy if h < PARTS - 1 else nc.vector.tensor_copy
+            interleave(
                 pg_bf[h][:].bitcast(F32).rearrange("p (z u) -> p z u", u=2),
                 pairs[h][:].rearrange("p u z e -> p (u z e)").bitcast(F32).rearrange("p (u z) -> p z u", u=2))
         scores = held("scores", [P, Z], F32)
-        for h in range(2):
-            codes = held("pg_codes_%d" % h, [P, HALF], U32)
-            plane = held("pg_plane_%d" % h, [P, HALF], U8)
+        banks = ["small0", "small1", "late0", "late1"]
+        for h in [0, 1, 3, 2]:
+            codes = held("pg_codes_%d" % h, [P, PART], U32)
+            plane = held("pg_plane_%d" % h, [P, PART], U8)
             nc.vector.quantize_mx(out=codes[:].bitcast(FP8X4), scales=plane[:], in_=pg_bf[h][:])
-            acc = ps.tile([P, HALF], F32, name="s_ps_%d" % h, tag="score%d" % h)
+            acc = ps.tile([P, PART], F32, name="s_ps_%d" % h, tag=banks[h])
             nc.tensor.matmul_mx(out=acc[:], lhsT=q_codes[:].bitcast(FP8X4), lhsT_scale=q_plane[:],
                                 rhs=codes[:].bitcast(FP8X4), rhs_scale=plane[:], start=True, stop=True)
-            zs = slice(h * HALF, (h + 1) * HALF)
-            if h == 0:
+            zs = slice(h * PART, (h + 1) * PART)
+            if h != 2:
                 nc.scalar.copy(scores[:, zs], acc[:])
             else:
                 nc.vector.tensor_copy(scores[:, zs], acc[:])
 
-        cols = J // 2 // 16
-        picked = [held("picked_%d" % h, [P, J // 2], F32) for h in range(2)]
-        for h in range(2):
-            nc.vector.tensor_copy(picked[h][:], scores[:].indirect(list3[:, h * cols:(h + 1) * cols]))
-            nc.scalar.activation(f3[:].indirect(list4[:, h * cols:(h + 1) * cols]), picked[h][:], COPY)
-        met = [held("met_%d" % h, [P, J // 2], F32) for h in range(2)]
-        nc.vector.tensor_copy(met[0][:], f3[:].indirect(list5[:, 0:cols]))
-        nc.scalar.activation(met[1][:], f3[:].indirect(list5[:, cols:2 * cols]), COPY)
+        def look_up(name, window, lst):
+            found = held(name, [P, J], F32)
+            cols = J // 2 // 16
+            nc.vector.tensor_copy(found[:, 0:J // 2], window[:].indirect(lst[:, 0:cols]))
+            nc.scalar.activation(found[:, J // 2:J], window[:].indirect(lst[:, cols:2 * cols]), COPY)
+            return found
+
+        picked = look_up("picked", scores, list3)
+        nc.scalar.activation(f3[:].indirect(list4[:]), picked[:], COPY)
+        met = look_up("met", f3, list5)
         result = held("result", [P, J], F32)
-        for h in range(2):
-            nc.vector.tensor_tensor(result[:, h * (J // 2):(h + 1) * (J // 2)], met[h][:], picked[h][:], MAX)
+        nc.vector.tensor_tensor(result[:], met[:], picked[:], MAX)
         nc.sync.dma_start(out, result[:])

from contextlib import ExitStack

import concourse.mybir as mybir

C, D, I, Z, J, Q = 512, 512, 256, 512, 256, 128
FLOPS = 2 * C * D * (Z + I + I) + 2 * D * Q * Z

F32 = mybir.dt.float32
BF16 = mybir.dt.bfloat16
I32 = mybir.dt.int32
U32 = mybir.dt.uint32
U16 = mybir.dt.uint16
U8 = mybir.dt.uint8
FP8X4 = mybir.dt.float8_e4m3fn_x4
FP4X4 = mybir.dt.float4_e2m1fn_x4
COPY = mybir.ActivationFunctionType.Copy
MAX = mybir.AluOpType.max
SUB = mybir.AluOpType.subtract

P = 128
PACK = 4
QUADS = 4
PARTS = 4
PART = Z // PARTS


def tile_attend_headmeet_plainq_kernel(tc, wp_words, wp_scales, olds_words, olds_scales, wk_words, wk_scales,
                                        news_words, news_scales, wl_words, wl_scales, lates_words, lates_scales,
                                        query, offs, offs2, offs3, offs4, offs5, out):
    nc = tc.nc
    with ExitStack() as ctx:
        sb = ctx.enter_context(tc.tile_pool(name="sb", bufs=1))
        ps = ctx.enter_context(tc.psum_pool(name="ps", bufs=1))

        def held(name, shape, dtype, tag=""):
            return sb.tile(shape, dtype, name=name, tag=tag or name, align_bytes=64)

        def load_list(name, src):
            lst = held(name, [P, 16], U16)
            nc.sync.dma_start(lst[:], src)
            return lst

        def load_words(name, src):
            words = held(name, [P, src.shape[1]], U8)
            nc.sync.dma_start(words[:].bitcast(I32), src.bitcast(I32))
            return words

        def dealt(ap):
            return ap.rearrange("p (g t w) -> p t g w", g=32, t=PACK)

        def by_place(ap, places=PACK):
            return ap.rearrange("p (t g w) -> p t g w", g=32, t=places)

        def deal(name, src):
            dst = held(name, [P, src.shape[1]], U8)
            nc.vector.tensor_copy(by_place(dst[:].bitcast(I32)), dealt(src[:].bitcast(I32)))
            return dst

        def zeroed(name, width, dtype, tag="", engine=nc.gpsimd):
            t = held(name, [P, width], dtype, tag)
            engine.memset(t[:].bitcast(I32), 0)
            return t

        def load_staged_scales(name, src):
            stage = held(name, [4, QUADS, src.shape[1] // 4], I32)
            nc.sync.dma_start(stage[:], src.bitcast(I32).rearrange("(u f) w -> f u w", f=4))
            return stage

        def load_scales(plane, src):
            for u in range(QUADS):
                nc.sync.dma_start(plane[32 * u: 32 * u + 4, :].bitcast(I32), src[4 * u: 4 * u + 4, :].bitcast(I32))

        def e4m3_rows(words):
            return words[0].rearrange("p n r -> p (n r)")

        warm = held("warm", [P, 16], F32)
        nc.vector.memset(warm[:, 0:8], 0.0)
        nc.scalar.activation(warm[:, 8:16], warm[:, 0:8], COPY)
        news_plane = zeroed("news_plane", 2 * I, U8)
        wk_stage = load_staged_scales("wk_stage", wk_scales[0])
        news_rows = news_scales[0].bitcast(I32).rearrange("(v u f) w -> u f v w", v=2, u=2)
        for u in range(2):
            nc.sync.dma_start(news_plane[32 * u:32 * u + 4, :].bitcast(I32).rearrange("f (v w) -> f v w", v=2),
                                news_rows[u])
        wk_raw = load_words("wk_raw", wk_words[0])
        news_w = load_words("news_w", e4m3_rows(news_words))
        list1 = load_list("list1", offs)

        wk_plane = zeroed("wk_plane", D, U8, engine=nc.vector)
        f1 = [zeroed("f1_%d" % t, Z, F32, engine=nc.vector) for t in range(2)]
        for u in range(QUADS):
            rows = slice(32 * u, 32 * u + 4)
            move, word = (nc.scalar.copy, U32) if u == 0 else (nc.vector.tensor_copy, I32)
            move(by_place(wk_plane[rows, :].bitcast(word)), dealt(wk_stage[:, u, :].bitcast(word)))
        nc.vector.tensor_copy(news_plane[64:P, 0:I].bitcast(I32), news_plane[0:64, I:2 * I].bitcast(I32))
        wk_w = held("wk_w", [P, 2 * D], U8)
        nc.scalar.copy(by_place(wk_w[:].bitcast(U32)), dealt(wk_raw[:].bitcast(U32)))
        f1.append(zeroed("f1_2", Z, F32, "wk_raw"))
        f1.append(zeroed("f1_3", Z, F32, "wk_stage"))

        def keys(acc, t, w_words, w_dtype, w_plane, x_words, x_dtype, x_plane):
            per = P * w_words.shape[1] // w_plane.shape[1]
            nc.tensor.matmul_mx(out=acc, lhsT=w_words[:, t * per:(t + 1) * per].bitcast(w_dtype),
                                lhsT_scale=w_plane[:, t * P:(t + 1) * P],
                                rhs=x_words[:].bitcast(x_dtype), rhs_scale=x_plane, start=True, stop=True)

        for t in range(PACK):
            acc = ps.tile([P, I], F32, name="kn_ps_%d" % t, tag="small%d" % (t % 2))
            keys(acc[:], t, wk_w, FP4X4, wk_plane, news_w, FP8X4, news_plane[:, 0:I])
            kn = held("kn_%d" % t, [P, I], F32)
            nc.vector.tensor_copy(kn[:], acc[:])
            nc.scalar.activation(f1[t][:].indirect(list1[:]), kn[:], COPY)

        wl_raw = load_words("wl_raw", e4m3_rows(wl_words))
        lates_w = load_words("lates_w", lates_words[0])
        list2 = load_list("list2", offs2)
        wl_plane_raw = zeroed("wl_plane_raw", D, U8)
        lates_plane = zeroed("lates_plane", I, U8)
        load_scales(wl_plane_raw, wl_scales[0])
        load_scales(lates_plane, lates_scales[0])

        q_raw = held("q_raw", [P, PACK, Q], F32)
        q_rows = query.rearrange("(g t e) q -> e g t q", t=PACK, e=4)
        for e in range(4):
            nc.sync.dma_start(q_raw[e:P:4, :, :], q_rows[e])

        wp_raw = load_words("wp_raw", e4m3_rows(wp_words))
        olds_w = load_words("olds_w", olds_words[0])
        wp_plane_raw = zeroed("wp_plane_raw", D, U8)
        olds_plane = zeroed("olds_plane", Z, U8)
        load_scales(wp_plane_raw, wp_scales[0])
        load_scales(olds_plane, olds_scales[0])
        list3 = load_list("list3", offs3)
        list4 = load_list("list4", offs4)
        list5 = load_list("list5", offs5)

        wl_w = deal("wl_w", wl_raw)
        wl_plane = deal("wl_plane", wl_plane_raw)
        f2 = [zeroed("f2_%d" % t, Z, F32, "kn_%d" % t) for t in range(PACK)]
        km = []
        for u in range(2):
            bank = ps.tile([P, 2 * I], F32, name="km_ps_%d" % u, tag="late%d" % u)
            for e in range(2):
                keys(bank[:, e * I:(e + 1) * I], 2 * u + e, wl_w, FP8X4, wl_plane, lates_w, FP4X4, lates_plane[:])
            km_pair = held("km_%d" % u, [P, 2 * I], F32)
            nc.vector.tensor_copy(km_pair[:], bank[:])
            km.extend([km_pair[:, 0:I], km_pair[:, I:2 * I]])

        q_bf = held("q_bf", [P, Q, PACK], BF16)
        nc.vector.tensor_copy(q_bf[:], q_raw[:].rearrange("p t q -> p q t"))
        wp_w = deal("wp_w", wp_raw)
        q_codes = held("q_codes", [P, Q], U32)
        q_plane = held("q_plane", [P, Q], U8)
        nc.vector.quantize_mx(out=q_codes[:].bitcast(FP8X4), scales=q_plane[:],
                              in_=q_bf[:].rearrange("p q t -> p (q t)"))
        wp_plane = deal("wp_plane", wp_plane_raw)
        f3 = zeroed("f3", Z, F32, "news_w")

        m1 = []
        for t in range(PACK):
            acc = ps.tile([P, Z], F32, name="kb_ps_%d" % t, tag="big%d" % t)
            keys(acc[:], t, wp_w, FP8X4, wp_plane, olds_w, FP4X4, olds_plane[:])
            m1.append(held("m1_%d" % t, [P, Z], F32))
            nc.vector.tensor_tensor(m1[t][:], acc[:], f1[t][:], MAX)

        pairs = [held("pairs_%d" % h, [P, 2, PART, 2], BF16) for h in range(PARTS)]
        for t in range(PACK):
            nc.scalar.activation(f2[t][:].indirect(list2[:]), km[t], COPY)
            for h in range(PARTS):
                zs = slice(h * PART, (h + 1) * PART)
                nc.vector.tensor_tensor(pairs[h][:, t // 2, :, t % 2], m1[t][:, zs], f2[t][:, zs], SUB)

        pg_bf = [held("pg_bf_%d" % h, [P, PART * PACK], BF16) for h in range(PARTS)]
        for h in range(PARTS):
            interleave = nc.scalar.copy if h < PARTS - 1 else nc.vector.tensor_copy
            interleave(
                pg_bf[h][:].bitcast(F32).rearrange("p (z u) -> p z u", u=2),
                pairs[h][:].rearrange("p u z e -> p (u z e)").bitcast(F32).rearrange("p (u z) -> p z u", u=2))
        scores = held("scores", [P, Z], F32)
        banks = ["small0", "small1", "late0", "late1"]
        for h in [0, 1, 3, 2]:
            codes = held("pg_codes_%d" % h, [P, PART], U32)
            plane = held("pg_plane_%d" % h, [P, PART], U8)
            nc.vector.quantize_mx(out=codes[:].bitcast(FP8X4), scales=plane[:], in_=pg_bf[h][:])
            acc = ps.tile([P, PART], F32, name="s_ps_%d" % h, tag=banks[h])
            nc.tensor.matmul_mx(out=acc[:], lhsT=q_codes[:].bitcast(FP8X4), lhsT_scale=q_plane[:],
                                rhs=codes[:].bitcast(FP8X4), rhs_scale=plane[:], start=True, stop=True)
            zs = slice(h * PART, (h + 1) * PART)
            if h != 2:
                nc.scalar.copy(scores[:, zs], acc[:])
            else:
                nc.vector.tensor_copy(scores[:, zs], acc[:])

        def look_up(name, window, lst):
            found = held(name, [P, J], F32)
            cols = J // 2 // 16
            nc.vector.tensor_copy(found[:, 0:J // 2], window[:].indirect(lst[:, 0:cols]))
            nc.scalar.activation(found[:, J // 2:J], window[:].indirect(lst[:, cols:2 * cols]), COPY)
            return found

        picked = look_up("picked", scores, list3)
        nc.scalar.activation(f3[:].indirect(list4[:]), picked[:], COPY)
        met = look_up("met", f3, list5)
        result = held("result", [P, J], F32)
        nc.vector.tensor_tensor(result[:], met[:], picked[:], MAX)
        nc.sync.dma_start(out, result[:])
